import numpy as np, ml_dtypes
CORES = [8,11,14,16,19,22,24,27,30]
N = 9
CB = 1
def setup_inputs(rng):
    k = (rng.standard_normal((N, 128, CB * 128), dtype=np.float32) / 8).astype(ml_dtypes.bfloat16)
    kt = np.concatenate([k[:, :, 128 * c:128 * c + 128].transpose(0, 2, 1) for c in range(CB)], axis=2)
    tri = np.triu(np.ones((128, 128), np.float32)).astype(ml_dtypes.bfloat16)
    return {"q": (rng.standard_normal((N, 128, CB * 128), dtype=np.float32) / 8).astype(ml_dtypes.bfloat16), "k": k, "kt": kt, "v": rng.standard_normal((N, 128, CB * 128), dtype=np.float32).astype(ml_dtypes.bfloat16), "m": np.broadcast_to(tri, (N, 128, 128)).copy()}
def setup_inputs_big(rng):
    d = setup_inputs(rng)
    for k in ("q", "k", "kt", "v"): d[k] = (d[k].astype(np.float32) * 1024.0).astype(d[k].dtype)
    return d
def setup_inputs_small(rng):
    d = setup_inputs(rng)
    for k in ("q", "k", "kt", "v"): d[k] = (d[k].astype(np.float32) * (1 / 1024.0)).astype(d[k].dtype)
    return d
def setup_inputs_apart(rng):
    d = setup_inputs(rng)
    f = (10.0 ** rng.permutation(np.linspace(-1.5, 1.5, N))).astype(np.float32).reshape(N, 1, 1)
    for k in ("q", "k", "kt", "v"): d[k] = (d[k].astype(np.float32) * f).astype(d[k].dtype)
    return d
def reference(q, k, kt, v, m):
    Q, K, KT, V, M = q.astype(np.float64), k.astype(np.float64), kt.astype(np.float64), v.astype(np.float64), m.astype(np.float64)
    y = np.zeros((N, 128, CB * 128)); Z = np.zeros((128, 128))
    for r in range(N):
        for c in range(CB):
            s = slice(128 * c, 128 * c + 128)
            y[r][:, s] = Z.T @ Q[r][:, s] + V[r][:, s].T @ ((K[r][:, s].T @ Q[r][:, s]) * M[r])
            Z = Z + KT[r][:, s].T @ V[r][:, s]
    return {"y": y.astype(ml_dtypes.bfloat16)}

from concourse.bass import DstId, RemoteDMATransfer
from concourse.mybir import AluOpType

P = 128
N = 9
NE = 8
BF = "bfloat16"

SCRATCH = {
    "kt_sb": ("sbuf", [P, P], BF), "v_sb": ("sbuf", [P, P], BF), "q_sb": ("sbuf", [P, P], BF),
    "k_sb": ("sbuf", [P, P], BF), "m_sb": ("sbuf", [P, P], BF),
    "am": ("sbuf", [P, P], BF),
    "yb": ("sbuf", [P, P], BF),
    "ps": ("psum", [P, 512], "float32"),
    "pa": ("psum", [P, 512], "float32"),
    "py": ("psum", [P, 512], "float32"),
}
for _r in range(N):
    SCRATCH["s%d" % _r] = ("sbuf", [P, P], BF)
    SCRATCH["c%d" % _r] = ("sbuf", [P, P], BF)

SEMAPHORES = ["ld_kv", "ld_qk", "ld_m", "mm_s", "cp_s", "mm_a", "cp_a", "mm_y", "cp_y", "st_y", "on", "sent"] + [
    "zc%d" % _r for _r in range(N)]


def _plan(cores, topo):
    groups = []
    for r, c in enumerate(cores):
        if groups and topo.chip(cores[groups[-1][-1]]) == topo.chip(c):
            groups[-1].append(r)
        else:
            groups.append([r])
    carry = []
    for grp in groups:
        load = dict((r, 0) for r in grp)
        car = {}
        for d in range(grp[-1] + 1, len(cores)):
            ok = [r for r in grp if topo.may_write(cores[r], cores[d])]
            b = min(ok, key=lambda r: (topo.die(cores[r]) != topo.die(cores[d]), load[r], r))
            load[b] += 1
            car.setdefault(b, []).append(d)
        carry.append(car)
    return groups, carry


def _first(mask, n):
    out, left = 0, n
    for b in range(mask.bit_length()):
        if left and (mask >> b) & 1:
            out |= 1 << b
            left -= 1
    return out


def rank_program(g, core, T, topo):
    rank = T.rank_of(core)
    if rank is None:
        return
    cores = list(T.cores)
    sem = T.sem
    te, ve = g.tensor, g.vector
    groups, carry = _plan(cores, topo)
    gi = [i for i, grp in enumerate(groups) if rank in grp][0]
    grp = groups[gi]

    def step1(s):
        return [d for d in grp if d != s and (d > s or d in carry[gi])]

    to1 = step1(rank)
    to2 = carry[gi].get(rank, [])
    n_on = NE * len([s for s in grp if s != rank and rank in step1(s)])
    mask = 0
    for d in to1 + to2:
        mask = topo.mask(core, cores[d]) if not mask else mask & topo.mask(core, cores[d])
    mask = _first(mask, NE)

    def ids(ranks):
        return [DstId(rid=topo.addr(cores[d])[0], pnc=topo.addr(cores[d])[1]) for d in ranks]

    n_kv = 16
    if to1:
        g.sync.dma_start(T.kt_sb[:], T.kt[:]).then_inc(sem.ld_kv, 16)
        n_kv = 32
    g.scalar.dma_start(T.v_sb[:], T.v[:]).then_inc(sem.ld_kv, 16)
    g.sync.dma_start(T.q_sb[:], T.q[:]).then_inc(sem.ld_qk, 16)
    g.scalar.dma_start(T.k_sb[:], T.k[:]).then_inc(sem.ld_qk, 16)
    g.sync.dma_start(T.m_sb[:], T.m[:]).then_inc(sem.ld_m, 16)

    own = T["s%d" % rank]
    te.wait_ge(sem.ld_kv, n_kv)
    if to1:
        te.matmul(T.ps[:, 0:P], T.kt_sb[:], T.v_sb[:], True, True).then_inc(sem.mm_s, 1)
        ve.wait_ge(sem.mm_s, 1)
        ve.tensor_copy(own[:], T.ps[:, 0:P]).then_inc(sem.cp_s, 1)

    sent = 0
    if to1:
        g.wait_ge(sem.cp_s, 1)
        g.remote_dma_fused([RemoteDMATransfer(dst_ids=ids(to1), dma_engine_mask=mask, remote_sem=sem.on,
                                              srcs=[own[:]], dsts=[own[:] for _ in to1], alu_op=0)],
                           local_sem=sem.sent)
        sent += NE
    if to2:
        g.wait_ge(sem.on, n_on)
        csum = T["c%d" % gi]
        g.remote_dma_fused([RemoteDMATransfer(dst_ids=ids(to2), dma_engine_mask=mask, remote_sem=sem["zc%d" % gi],
                                              srcs=[T["s%d" % s][:] for s in grp], dsts=[csum[:] for _ in to2],
                                              alu_op=1)],
                           local_sem=sem.sent)
        sent += NE

    te.wait_ge(sem.ld_qk, 32)
    te.matmul(T.pa[:, 0:P], T.k_sb[:], T.q_sb[:], True, True).then_inc(sem.mm_a, 1)
    ve.wait_ge(sem.mm_a, 1)
    ve.wait_ge(sem.ld_m, 16)
    ve.tensor_tensor(T.am[:], T.pa[:, 0:P], T.m_sb[:], AluOpType.mult).then_inc(sem.cp_a, 1)
    te.wait_ge(sem.cp_a, 1)

    near = [s for s in grp if s < rank]
    far = list(range(gi - 1, -1, -1))
    left = len(near) + len(far)
    mm = te.matmul(T.py[:, 0:P], T.v_sb[:], T.am[:], True, left == 0)
    if near:
        te.wait_ge(sem.on, n_on)
    for s in near:
        left -= 1
        mm = te.matmul(T.py[:, 0:P], T["s%d" % s][:], T.q_sb[:], False, left == 0)
    for c in far:
        te.wait_ge(sem["zc%d" % c], NE)
        left -= 1
        mm = te.matmul(T.py[:, 0:P], T["c%d" % c][:], T.q_sb[:], False, left == 0)
    mm.then_inc(sem.mm_y, 1)
    ve.wait_ge(sem.mm_y, 1)
    ve.tensor_copy(T.yb[:], T.py[:, 0:P]).then_inc(sem.cp_y, 1)
    g.sync.wait_ge(sem.cp_y, 1)
    g.sync.dma_start(T.y[:], T.yb[:]).then_inc(sem.st_y, 16)
    g.sync.wait_ge(sem.st_y, 16)
    if sent:
        g.wait_ge(sem.sent, sent)
